import numpy as np, ml_dtypes
CORES = [2,3,42,43,82,83,122,123]
N = 8
BF = ml_dtypes.bfloat16
W, K, T, S, ND = 4096, 256, 3, 3, 3
def stir(rng, a, n):
    r = rng.random(a.shape, dtype=np.float32)
    s = np.concatenate([np.sort(r, axis=-1), np.full(r.shape[:-1] + (1,), 2, np.float32)], axis=-1)
    return np.where(r < np.take_along_axis(s, n[..., None], -1), (a + rng.integers(1, 64, a.shape)) & 63, a)
def near(rng, pro, n, counts):
    a = pro[np.arange(8)[None, :, None], rng.integers(0, pro.shape[1], (N, 8, n))]
    return stir(rng, a, rng.choice(np.array(counts), (N, 8, n)))
def protos(rng, first):
    return stir(rng, np.repeat(first, 2, axis=1), np.full((8, 2), 3))
def parts(rng):
    pro = protos(rng, rng.integers(0, 64, (8, 1, 16)))
    return (near(rng, pro, K, [0, 1, 1, 2, 2, 3, 16]), rng.integers(0, 256, (N, 8, K, 16)), near(rng, pro, W, [0, 1, 1, 2, 3, 16]), rng.integers(0, 256, (N, 8, W, 16)),
            rng.integers(0, 256, (8, 16, 2)), rng.integers(900, 1900, (N, 8, 16)))
def tile(a):
    return np.ascontiguousarray(a.transpose(0, 1, 3, 2)).reshape(N, 128, -1).astype(np.float32).astype(BF)
def pack(x, g, lx, lm, w, lim):
    return {"xw": tile(x), "gw": tile(g), "lex": tile(lx), "mng": tile(lm),
            "wts": np.ascontiguousarray(np.broadcast_to(w.reshape(1, 128, 2), (N, 128, 2))).astype(np.int32), "th": lim.reshape(N, 128, 1).astype(np.int32)}
def setup_inputs(rng):
    return pack(*parts(rng))
def setup_inputs_spread(rng):
    pro = protos(rng, (64 * rng.random((8, 1, 16)) ** 3).astype(np.int64))
    x = near(rng, pro, K, [0, 1, 1, 2, 3, 4, 16]); lx = near(rng, pro, W, [0, 1, 1, 2, 4, 16])
    g = np.floor(256 * rng.random((N, 8, K, 1)) ** 2 * rng.random((N, 8, K, 16))).astype(np.int64)
    lm = np.floor(256 * rng.random((N, 8, W, 1)) ** 2 * rng.random((N, 8, W, 16))).astype(np.int64)
    w = np.exp2(8 * rng.random((8, 16, 2))).astype(np.int64) - 1; w = np.where(rng.random(w.shape) < 0.25, rng.integers(0, 256, w.shape), w)
    lim = np.minimum(np.exp2(4 + 8.2 * rng.random((N, 8, 16))).astype(np.int64), 4081)
    return pack(x, g, lx, lm, w, lim)
def setup_inputs_ends(rng):
    base = np.repeat(63 * rng.integers(0, 2, (8, 1, 16)), 2, axis=1); base[:, 1] = np.where(rng.random((8, 16)) < 0.15, 63 - base[:, 1], base[:, 1])
    def some(n, share):
        a = base[np.arange(8)[None, :, None], rng.integers(0, 2, (N, 8, n))]
        return np.where(rng.random(a.shape) < share, np.where(rng.random(a.shape) < 0.6, 63 - a, rng.choice(np.array([1, 31, 62]), a.shape)), a)
    def both(n):
        return 255 * np.where(rng.random((N, 8, n, 1)) < 0.5, rng.integers(0, 2, (N, 8, n, 1)), rng.integers(0, 2, (N, 8, n, 16)))
    x = some(K, 0.08); lx = some(W, 0.1); g = both(K); lm = both(W)
    w = 255 * rng.integers(0, 2, (8, 16, 2)); w[:5, 15] = 65; w[5, :, 0] = 255; w[6, 0] = 65; w[7, 14:, 0] = 65; w[7, 14:, 1] = 0
    w[4, 13, 0] = 89; w[4, 13, 1] = 0; w[4, 14, 0] = 0; w[4, 14, 1] = 227
    lim = np.full((N, 8, 16), 4081); odd = np.arange(N) % 2 == 1
    lim = np.where(odd[:, None, None] & (rng.random(lim.shape) < 0.25), 0, lim); lim[:, 0, 0] = 0
    x[:, 0, :, 0] = 63; lx[:, 0, :, 0] = 63
    x[:, 5, 1] = 63; x[:, 5, K - 1] = 63
    for i in (3, K - 2):
        x[:, 1:5, i] = 0; x[:, 1:5, i, 15] = 63
    p = (((W - 1) ** 2 >> 5) + W - 1) & (W - 1)
    lx[:, 1:5, p] = 0; lx[:, 1:5, p, 15] = 63; lx[:, 1:5, p, 13] = 63
    x[:, 4, 4] = 0; x[:, 4, 4, 13] = 46; x[:, 4, 4, 14] = 36; x[:, 4, 4, 15] = 63
    p = ((4093 * 4075 >> 5) + 4093) & (W - 1)
    lx[:, 4, p] = x[:, 4, 4]; lx[:, 4, p, 0] = 63; lx[:, 4, p + 1] = 63; lm[:, 4, p] = 255; g[:, 4, 4] = 0
    x[:, 7, 4] = 0; x[:, 7, 4, 14] = 63; g[:, 7, 4] = 0
    for i in (5, K - 1):
        x[:, 7, i] = 0; x[:, 7, i, 15] = 63; g[:, 7, i] = 255 if i == 5 else 0
    lx[:, 7, 0] = 63; lx[:, 7, W - 1] = 0; lx[:, 7, W - 1, 14:] = 63; lm[:, 7, W - 1] = 255
    g[:, 6, :, 15] = 255; lm[:, 6, :, 15] = 255; g[:, 6, :, 14] = 0; lm[:, 6, :, 14] = 0
    return pack(x, g, lx, lm, w, lim)
def setup_inputs_corners(rng):
    pro = rng.integers(0, 64, (8, 1, 16)); lx = near(rng, pro, W, [0, 0, 1]); lx[:, :, 0] = pro[:, 0]
    x = near(rng, pro, K, [0, 1, ND, ND + 1, ND + 2, 16])
    w = rng.integers(0, 256, (8, 16, 2)); w[0] = 0; w[1] = 255; w[2, :, 0] = 0; w[2, :, 1] = 255; w[3, :, 1] = w[3, :, 0]; w[4, :15] = 0; w[4, 15] = 255; w[5, 1:] = 0; w[5, 0] = 255
    w[6] = 255 * rng.integers(0, 2, (16, 2)); w = w[rng.permutation(8)]
    def mean(n):
        return np.where(rng.random((N, 8, n, 1)) < 0.6, 255 * rng.integers(0, 2, (N, 8, n, 1)), rng.integers(0, 256, (N, 8, n, 16)))
    case = (np.arange(8)[None, :] + np.arange(N)[:, None] + rng.integers(0, 5)) % 5; case = case[:, :, None]
    lim = np.where(case == 0, 0, np.where(case == 1, 4081, np.where(case == 2, 4081 * rng.integers(0, 2, (N, 8, 16)), np.where(case == 3, 1, rng.integers(900, 1900, (N, 8, 16))))))
    return pack(x, mean(K), lx, mean(W), w, lim)
def setup_inputs_ties(rng):
    pro = rng.integers(0, 64, (8, 1, 16)); far = np.where(rng.permutation(8) < 4, 0, rng.integers(130, 251, 8)).reshape(8, 1, 1)
    b = rng.integers(0, 255 - far, (8, 1, 16)); side = rng.integers(0, 2, (8, 1, 16))
    x = near(rng, pro, K, [0, 1, 1, 1]); lx = near(rng, pro, W, [0, ND, ND, ND + 1])
    g = b + far * side + rng.integers(0, 2, (N, 8, K, 16)); lm = b + far * (1 - side) + rng.integers(0, 2, (N, 8, W, 16))
    lim = np.where(far[:, 0] == 0, rng.integers(5, 13, (N, 8, 16)), 16 * far[:, 0] + rng.integers(-3, 5, (N, 8, 16)))
    return pack(x, g, lx, lm, rng.integers(0, 256, (8, 16, 2)), lim)
def setup_inputs_alike(rng):
    o = rng.permutation(64); al = o[:4]; kinds = (rng.integers(0, 4, (8, 1, 16)) + (rng.random((8, 6, 16)) < 0.12) * rng.integers(1, 4, (8, 6, 16))) & 3
    pro = al[kinds]; x = near(rng, pro, K, [0]); lx = near(rng, pro, W, [0])
    g = rng.integers(0, 256, (N, 8, K, 16)); lm = rng.integers(0, 256, (N, 8, W, 16)); w = rng.integers(0, 256, (8, 16, 2))
    even = (np.arange(N) % 2 == 0)[:, None, None]
    lim = np.where((rng.random((N, 8, 1)) < 0.6) | even, 4081, rng.integers(900, 1900, (N, 8, 16)))
    two = np.sort(o[4:12].reshape(4, 2), axis=1); spot = np.arange(W); four = [int(e) for e in rng.permutation(8)[:4]]
    for e in four:
        lx[:, e] = pro[e, 0]; lx[:, e, :, 0] = two[spot & 3, 1]; lx[:, e, :, 14] = spot & 63; lx[:, e, :, 15] = spot >> 6
        w[e] = 0; w[e, 14, 0] = 1; w[e, 15, 0] = 64; lim[:, e] = 4081
    for r in range(N):
        j = rng.permutation(W >> 1)[:K]
        put = [4 * (j >> 1) + 2 + (j & 1),
               np.full(K, 4 * rng.integers(0, W >> 2) + 2 + rng.integers(0, 2)),
               4 * rng.permutation(W >> 2)[:K] + (np.arange(K) >= 256),
               np.repeat(4 * rng.permutation(W >> 2)[:K >> 1] + (np.arange(K >> 1) & 3), 2)]
        for e, p in zip(four, put):
            x[r, e] = pro[e, 0]; x[r, e, :, 0] = two[p & 3, 0]; x[r, e, :, 14] = p & 63; x[r, e, :, 15] = p >> 6
    e = four[2]
    g[:, e] = rng.integers(0, 41, (N, K, 16)) + 200 * even; lm[:, e] = rng.integers(0, 41, (N, W, 16)); lim[:, e] = rng.integers(700, 2500, (N, 16))
    return pack(x, g, lx, lm, w, lim)
def check_inputs(d):
    bad = []
    for k, lo, hi in (("xw", 0, 63), ("gw", 0, 255), ("lex", 0, 63), ("mng", 0, 255), ("wts", 0, 255), ("th", 0, 4081)):
        a = np.asarray(d[k]).astype(np.float64)
        if not (np.min(a) >= lo and np.max(a) <= hi): bad.append("range of " + k)
        elif np.any(a != np.floor(a)): bad.append("whole numbers of " + k)
    a = np.asarray(d["wts"])
    if np.any(a != a[:1]): bad.append("wts alike on all ranks")
    return bad
def visit(t, x, g, lx, lm, w, lim):
    p = w[..., :1] * x; u = (np.add.reduce(p, axis=1, keepdims=True) - p) & (W - 1)
    p = w[..., 1:] * x; u2 = (np.add.reduce(p, axis=1, keepdims=True) - p) & (W - 1)
    h = (((u * u2) >> 5) + u) & (W - 1)
    c = np.take_along_axis(lx, h.reshape(8, 1, 16 * K), 2).reshape(8, 16, 16, K)
    m = np.take_along_axis(lm, h.reshape(8, 1, 16 * K), 2).reshape(8, 16, 16, K)
    differ = np.add.reduce((c != x[:, :, None, :]).astype(np.int32), axis=1)
    far = np.add.reduce(np.abs(m - g[:, :, None, :]), axis=1)
    lane = np.arange(16); b = c[:, lane, lane, :]
    pair = (b != x) & (differ <= ND + 1)
    has = np.any(pair, axis=1); f = np.argmax(pair, axis=1)[:, None, :]
    def at(a):
        return np.take_along_axis(a, f, 1)[:, 0]
    xa, xb, hf = at(x), at(b), at(h)
    free = at((far < lim).astype(np.int32)) == 1
    pc = 64 * np.minimum(xa, xb) + np.maximum(xa, xb)
    flag = np.zeros(4096, bool); flag[pc[has & ~free]] = True
    merge = has & free & ~flag[pc]
    mf = np.take_along_axis(lm, hf[:, None, :], 2)
    row = lane[None, :, None]
    xn = np.where((row == f) & merge[:, None, :], np.minimum(x, b), x)
    xn = np.where((row == t) & ~has[:, None, :], b, xn)
    gn = np.where(merge[:, None, :], (g + mf) >> 1, g)
    for e in range(8):
        for i in np.flatnonzero(merge[e])[::-1]:
            lx[e, :, hf[e, i]] = xn[e, :, i]; lm[e, :, hf[e, i]] = gn[e, :, i]
    x[...] = xn; g[...] = gn
def reference(xw, gw, lex, mng, wts, th):
    x = xw.astype(np.float32).astype(np.int32).reshape(N, 8, 16, K); g = gw.astype(np.float32).astype(np.int32).reshape(N, 8, 16, K)
    lx = lex.astype(np.float32).astype(np.int32).reshape(N, 8, 16, W); lm = mng.astype(np.float32).astype(np.int32).reshape(N, 8, 16, W)
    w = wts.astype(np.int32).reshape(N, 8, 16, 2); lim = th.astype(np.int32).reshape(N, 8, 16, 1)
    for t in range(T):
        for r in range(N):
            v = (r + S * t) % N; visit(t, x[r], g[r], lx[v], lm[v], w[v], lim[v])
    return {"yx": x.reshape(N, 128, K).astype(np.float32).astype(BF), "yg": g.reshape(N, 128, K).astype(np.float32).astype(BF),
            "yl": lx.reshape(N, 128, W).astype(np.float32).astype(BF), "ym": np.add.reduce(lm, axis=3).reshape(N, 128, 1).astype(np.float32)}

from concourse.mybir import AluOpType, AxisListType, ActivationFunctionType

OP = AluOpType
AF = ActivationFunctionType
W, K = 4096, 256

_S = {}


def _sb(name, cols, dtype="bfloat16"):
    _S[name] = ("sbuf", [128, cols], dtype)


_sb("LX", W + K)
_sb("LM", W + K)
for _n in ("X0", "M0", "X1", "M1", "X2", "M2", "X3", "M3", "XN0", "XN1", "XN2", "MN0", "MN1", "MN2"):
    _sb(_n, K)
for _n in ("MG", "MI"):
    _sb(_n, 128, "float32")
_sb("PI", 4, "int32")
_sb("PF", 8, "float32")
_sb("THR", 4, "float32")
_sb("SQB", 1, "float32")
_sb("WI", 2, "int32")
_sb("WF", 2, "float32")
_sb("THI", 1, "int32")
_sb("THF", 1, "float32")
_CB = ("BO", "BO64", "BO8192", "ID", "IDN", "ID2", "IDN128", "ID128", "ID64", "ID8192", "SL", "MNE", "BOX", "W1", "W2",
       "BASE", "C2", "LT0", "LT1", "LT2", "BN8")
for _n in _CB:
    _sb(_n, 128)
for _n in ("BOH", "IDH", "THB"):
    _sb(_n, 128, "float16")
_sb("SK", 2048)
_sb("RXI", 512, "float32")
_sb("RX", 512)
_sb("IO64", 64)
_S["TRI"] = ("sbuf", [128, 16, 16], "bfloat16")
_S["TRII"] = ("sbuf", [128, 256], "float32")
_sb("IDX0", 16, "float32")
_sb("IDX2", 16, "float32")
_sb("QB", 144)
_sb("Q512", 144)
_sb("QH", 144, "float16")
_sb("Q16", 144, "float16")
_sb("UI", 512, "int32")
_sb("PR", 256, "int32")
_sb("HQ", 256, "int32")
_sb("HI", 256, "int32")
_sb("HU", 256, "uint16")
_sb("H16", 256, "float16")
_sb("CB", 4096)
_sb("EB", 4096)
_sb("PB", 256)
_sb("FB", 256, "float16")
_sb("FH", 256, "float16")
_sb("FX", 256)
_sb("FC", 256)
_sb("NH", 256)
_sb("XA", 256)
_sb("LF", 16, "uint16")
_sb("SUB", 256)
_sb("ABS", 256)
_sb("XTS", 16, "float32")
_sb("CTS", 16, "float32")
_sb("NTS", 16, "float32")
_sb("OHX", 1024)
_sb("OHC", 1024)
_sb("XL", 16, "int32")
_sb("XLF", 16, "float32")
_sb("CLF", 16, "float32")
_sb("CL", 16, "uint16")
_sb("SQ", 256)
_sb("MK", 256)
_sb("TB", 64)
_sb("TW", 256)
_sb("HN", 256)
_sb("GT", 256)
_sb("DMI", 256, "int32")
_sb("DM", 256)
_sb("MGR", 256)
_sb("DT", 256)
_sb("DK", 256, "float16")
_sb("KLS", 16, "float32")
_S["EQ"] = ("sbuf", [128, 16, 256], "bfloat16")
_sb("LS", 256)
_sb("OFF", 16, "float32")
_sb("OFU", 16, "uint16")
_sb("SUM", 4, "float32")
_sb("YM", 1, "float32")
for _i in range(8):
    _S["B%d" % _i] = ("psum", [128, 512], "float32")
SCRATCH = _S
SEMAPHORES = (["qv", "qs", "qt", "qg", "ls"] + ["d%d" % _i for _i in range(12)]
              + ["ax%d" % _i for _i in range(1, 4)] + ["am%d" % _i for _i in range(1, 4)])


def rank_program(g, core, T, topo):
    rank = T.rank_of(core)
    if rank is None:
        return
    n_ranks = len(T.cores)
    que = {"v": g.vector, "s": g.scalar, "t": g.tensor, "g": g, "y": g.sync}
    clock = {q: {} for q in que}
    count = {"qv": 0, "qs": 0, "qt": 0, "qg": 0}
    lastw, readers, touch = {}, {}, {}
    dmas = []

    def wait(q, tok):
        sem, n, snap = tok[0], tok[1], tok[2]
        if clock[q].get(sem, 0) >= n:
            return
        que[q].wait_ge(T.sem[sem], n)
        for s, m in snap.items():
            if clock[q].get(s, 0) < m:
                clock[q][s] = m
        clock[q][sem] = n

    def before(q, reads, writes, dma=False):
        toks = {}

        def need(tok):
            if tok[0] not in toks or toks[tok[0]][1] < tok[1]:
                toks[tok[0]] = tok
        for k in reads:
            if k in lastw:
                need(lastw[k])
        for k in writes:
            if k in lastw and (dma or lastw[k][3] != q):
                need(lastw[k])
            for tok in readers.get(k, {}).values():
                if dma or tok[3] != q:
                    need(tok)
        for k in list(reads) + list(writes):
            for e, tok in touch.get(k, {}).items():
                if e != q:
                    need(tok)
        for tok in toks.values():
            wait(q, tok)

    def after(tok, reads, writes):
        for k in writes:
            lastw[k] = tok
            readers[k] = {}
        for k in reads:
            if k not in writes:
                readers.setdefault(k, {})[tok[0]] = tok
        for k in list(reads) + list(writes):
            if k in BANKS:
                touch.setdefault(k, {})[tok[3]] = tok

    BANKS = ["B%d" % i for i in range(8)]

    def do(q, reads, writes, name, **kw):
        before(q, reads, writes)
        sem = "q" + q
        count[sem] += 1
        ins = None
        if name == "copy":
            ins = g.vector.tensor_copy(**kw)
        elif name == "tt":
            ins = g.vector.tensor_tensor(**kw)
        elif name == "ts":
            ins = g.vector.tensor_scalar(**kw)
        elif name == "act":
            ins = g.scalar.activation(**kw)
        elif name == "mm":
            ins = g.tensor.matmul(kw["out"], kw["l"], kw["r"], kw["start"], kw["stop"])
        elif name == "fill":
            ins = g.vector.memset(kw["ap"], kw["c"])
        elif name == "iota":
            ins = g.iota(**kw)
        elif name == "reduce":
            ins = g.vector.tensor_reduce(**kw)
        ins.then_inc(T.sem[sem], 1)
        after((sem, count[sem], dict(clock[q]), q), reads, writes)

    def dma(q, out, in_, reads, writes):
        before(q, reads, writes, True)
        sem = "d%d" % len(dmas)
        que[q].dma_start(out, in_).then_inc(T.sem[sem], 16)
        tok = (sem, 16, dict(clock[q]), "dma")
        dmas.append(tok)
        after(tok, reads, writes)

    def cp(out, in_, r, w):
        do("v", r, w, "copy", out=out, in_=in_)

    def tt(out, a, b, op, r, w):
        do("v", r, w, "tt", out=out, in0=a, in1=b, op=op)

    def ts(out, a, s1, op0, r, w, s2=None, op1=None):
        if op1 is None:
            do("v", r, w, "ts", out=out, in0=a, scalar1=s1, scalar2=None, op0=op0)
        else:
            do("v", r, w, "ts", out=out, in0=a, scalar1=s1, scalar2=s2, op0=op0, op1=op1)

    def act(out, in_, r, w, func=AF.Copy, **kw):
        do("s", r, w, "act", out=out, in_=in_, func=func, **kw)

    def mm(out, l, r, start, stop, rd, wr):
        do("t", rd, wr, "mm", out=out, l=l, r=r, start=start, stop=stop)

    def iota(out, pattern, base, cm, w, small=True):
        if small:
            do("g", [], w, "iota", out=out, pattern=pattern, base=base, channel_multiplier=cm,
               allow_small_or_imprecise_dtypes=True)
        else:
            do("g", [], w, "iota", out=out, pattern=pattern, base=base, channel_multiplier=cm)

    dma("y", T.X0[:], T.xw[:], [], ["X0"])
    dma("s", T.WI[:], T.wts[:], [], ["WI"])
    dma("y", T.LX[:, 0:W], T.lex[:], [], ["LX"])
    dma("s", T.THI[:], T.th[:], [], ["THI"])
    dma("y", T.M0[:], T.gw[:], [], ["M0"])
    dma("y", T.LM[:, 0:W], T.mng[:], [], ["LM"])

    iota(T.PI[:, 0:1], [[0, 1]], 0, 1, ["PI"], False)
    iota(T.MG[:], [[1, 8], [0, 16]], 0, 0, ["MG"])
    iota(T.MI[:], [[1, 128]], 0, 0, ["MI"])
    iota(T.IO64[:], [[1, 64]], 0, 0, ["IO64"])
    iota(T.IDX0[:], [[16, 16]], 2048, 0, ["IDX0"])
    iota(T.TRII[:], [[0, 16], [1, 16]], 0, 0, ["TRII"])
    iota(T.RXI[:], [[1, 4], [0, 8], [4, 16]], 0, 0, ["RXI"])
    do("v", [], ["SK"], "fill", ap=T.SK[:], c=0.0)
    for nm in ("QB", "Q512"):
        do("v", [], [nm], "fill", ap=T[nm][:], c=0.0)
    ts(T.PI[:, 1:2], T.PI[:, 0:1], 4, OP.arith_shift_right, ["PI"], ["PI1"])
    ts(T.PI[:, 2:3], T.PI[:, 0:1], 15, OP.bitwise_and, ["PI"], ["PI2"])
    cp(T.PF[:, 0:3], T.PI[:, 0:3], ["PI", "PI1", "PI2"], ["PF"])
    pI, pG, pL = T.PF[:, 0:1], T.PF[:, 1:2], T.PF[:, 2:3]
    ts(T.BO[:], T.MG[:], pG, OP.is_equal, ["MG", "PF"], ["BO"])
    ts(T.ID[:], T.MI[:], pI, OP.is_equal, ["MI", "PF"], ["ID"])
    cp(T.WF[:], T.WI[:], ["WI"], ["WF"])
    tt(T.MNE[:], T.BO[:], T.ID[:], OP.subtract, ["BO", "ID"], ["MNE"])
    ts(T.W1[:], T.MNE[:], T.WF[:, 0:1], OP.mult, ["MNE", "WF"], ["W1"])
    ts(T.W2[:], T.MNE[:], T.WF[:, 1:2], OP.mult, ["MNE", "WF"], ["W2"])
    act(T.IDH[:], T.ID[:], ["ID"], ["IDH"])
    act(T.BOH[:], T.BO[:], ["BO"], ["BOH"])
    for nm, src, f in (("IDN", "ID", -1.0), ("ID2", "ID", 2.0), ("IDN128", "ID", -128.0), ("ID128", "ID", 128.0),
                       ("ID64", "ID", 64.0), ("ID8192", "ID", 8192.0), ("BO64", "BO", 64.0), ("BO8192", "BO", 8192.0),
                       ("BN8", "BO", -8.0)):
        act(T[nm][:], T[src][:], [src], [nm], scale=f)

    def later_constants():
        ts(T.C2[:], T.ID[:], 16.0, OP.mult, ["ID"], ["C2"])
        tt(T.BOX[:], T.BO[:], T.C2[:], OP.subtract, ["BO", "C2"], ["BOX"])
        for e in range(8):
            cp(T.SK[:, 16 * e:16 * e + 129 * 15 + 1:129], T.BOX[:, 16 * e:16 * e + 16], ["BOX"], ["SK"])
        ts(T.SL[:], T.MI[:], pI, OP.is_gt, ["MI", "PF"], ["SL"])
        tt(T.SL[:], T.SL[:], T.BO[:], OP.mult, ["SL", "BO"], ["SL"])
        tt(T.BASE[:], T.SL[:], T.ID[:], OP.subtract, ["SL", "ID"], ["BASE"])
        ts(T.C2[:], T.SL[:], 31.0, OP.mult, ["SL"], ["C2"])
        tt(T.C2[:], T.C2[:], T.BO[:], OP.add, ["C2", "BO"], ["C2"])
        ts(T.LT1[:], T.ID[:], 17.0, OP.mult, ["ID"], ["LT1"])
        tt(T.C2[:], T.C2[:], T.LT1[:], OP.subtract, ["C2", "LT1"], ["C2"])
        for t in range(3):
            nm = "LT%d" % t
            cp(T[nm][:], T.BASE[:], ["BASE", "C2"], [nm])
            cp(T[nm][:, t::16], T.C2[:, t::16], ["C2", nm], [nm])
            ts(T.THR[:, t:t + 1], pL, float(t), OP.not_equal, ["PF"], ["THR"], -0.5, OP.mult)
        cp(T.QB[:, 15:128:16], T.BO[:, ::16], ["BO"], ["QB"])
        ts(T.Q512[:, 15:128:16], T.BO[:, ::16], 512.0, OP.mult, ["BO"], ["Q512"])
        cp(T.QH[:], T.QB[:], ["QB"], ["QH"])
        ts(T.Q16[:], T.QB[:], 0.0625, OP.mult, ["QB"], ["Q16"])
        ts(T.THF[:], T.THI[:], -1.0, OP.mult, ["THI"], ["THF"], 2048.0, OP.add)
        ts(T.THB[:], T.BO[:], T.THF[:], OP.mult, ["BO", "THF"], ["THB"])
        ts(T.SQB[:], pL, -4.0, OP.mult, ["PF"], ["SQB"], -1.5, OP.add)
        ts(T.IDX2[:], T.IDX0[:], pL, OP.add, ["IDX0", "PF"], ["IDX2"])
        ts(T.RX[:], T.RXI[:], pI, OP.is_equal, ["RXI", "PF"], ["RX"])
        for c in range(16):
            ts(T.TRI[:, c, :], T.TRII[:, 16 * c:16 * c + 16], pL, OP.is_gt, ["TRII", "PF"], ["TRI"])

    def qwin(name, p):
        return T[name][:, 15 - p:143 - p]

    deferred = []
    for t in range(3):
        xn, mn = "XN%d" % t, "MN%d" % t
        X, M = "X%d" % t, "M%d" % t
        TX, TM = T[X], T[M]
        for h in range(2):
            for j, w in ((0, "W1"), (1, "W2")):
                mm(T.B0[:, 256 * h + 128 * j:256 * h + 128 * j + 128], T[w][:], TX[:, 128 * h:128 * h + 128], True, True,
                   [w, X], ["B0"])
        mm(T.B1[:, 0:256], T.ID[:], TX[:], True, True, ["ID", X], ["B1"])

        def hashes(h):
            a, b = 256 * h, 128 * h
            ui, pr, hq, hi = ("UI", h), ("PR", h), ("HQ", h), ("HI", h)
            cp(T.UI[:, a:a + 256], T.B0[:, a:a + 256], ["B0"], [ui])
            ts(T.UI[:, a:a + 256], T.UI[:, a:a + 256], 4095, OP.bitwise_and, [ui], [ui])
            tt(T.PR[:, b:b + 128], T.UI[:, a:a + 128], T.UI[:, a + 128:a + 256], OP.mult, [ui], [pr])
            ts(T.HQ[:, b:b + 128], T.PR[:, b:b + 128], 5, OP.arith_shift_right, [pr], [hq])
            tt(T.HQ[:, b:b + 128], T.HQ[:, b:b + 128], T.B0[:, a:a + 128], OP.add, [hq, "B0"], [hq])
            ts(T.HI[:, b:b + 128], T.HQ[:, b:b + 128], 4095, OP.bitwise_and, [hq], [hi])
            cp(T.HU[:, b:b + 128], T.HI[:, b:b + 128], [hi], [("HU", h)])

        def sgather(w0, w1, key):
            act(T.CB[:, 16 * w0:16 * w1], T.LX[:, 0:W].indirect(T.HU[:, w0:w1]), ["LX", ("HU", w0 // 128)], [key])

        hashes(0)
        sgather(0, 64, ("CB", 0))
        sgather(64, 128, ("CB", 1))
        hashes(1)
        sgather(128, 192, ("CB", 2))
        sgather(192, 224, ("CB", 3))
        if t == 0:
            later_constants()
        cp(T.CB[:, 3584:4096], T.LX[:, 0:W].indirect(T.HU[:, 224:256]), ["LX", ("HU", 1)], [("CB", 4)])
        for f in deferred:
            f()
        deferred = []
        ts(T.H16[:], T.HI[:], -2048.0, OP.add, [("HI", 0), ("HI", 1)], ["H16"])
        mm(T.B7[:, 256:512], T.IDH[:], T.H16[:], True, True, ["IDH", "H16"], ["B7"])
        for c in range(4):
            for k in range(16):
                o = 1024 * c
                tt(T.EB[:, o + 64 * k:o + 64 * k + 64], T.CB[:, o + k:o + 1024:16], T.B1[:, 64 * c:64 * c + 64], OP.not_equal,
                   [("CB", c), "B1"] + ([("CB", 4)] if c == 3 else []), [("EB", c, k // 4)])
            for k in range(16):
                mm(T.B2[:, 64 * c:64 * c + 64], T.SK[:, 128 * k:128 * k + 128], T.EB[:, 1024 * c + 64 * k:1024 * c + 64 * k + 64],
                   k == 0, k == 15, ["SK", ("EB", c, k // 4)], ["B2"])
        ts(T.PB[:], T.B2[:, 0:256], -11.5, OP.is_le, ["B2"], ["PB"])
        lt = "LT%d" % t
        mm(T.B2[:, 256:512], T[lt][:], T.PB[:], True, True, [lt, "PB"], ["B2"])
        mm(T.B3[:, 256:512], T.BO[:], T.PB[:], True, True, ["BO", "PB"], ["B3"])
        ts(T.FB[:], T.B2[:, 256:512], T.THR[:, t:t + 1], OP.is_le, ["B2", "THR"], ["FB"])
        tt(T.FH[:], T.FB[:], T.B7[:, 256:512], OP.mult, ["FB", "B7"], ["FH"])
        for p in range(16):
            mm(T.B4[:, 0:16], qwin("QH", p), T.FH[:, p::16], p == 0, p == 15, ["QH", "FH"], ["B4"])
        tt(T.FX[:], T.FB[:], T.B1[:, 0:256], OP.mult, ["FB", "B1"], ["FX"])
        ts(T.NH[:], T.B3[:, 256:512], 0.5, OP.is_le, ["B3"], ["NH"], 64.0, OP.mult)
        tt(T.XA[:], T.NH[:], T.B1[:, 0:256], OP.add, ["NH", "B1"], ["XA"])
        for h in range(2):
            mm(T.B2[:, 8 * h:8 * h + 8], T.FX[:, 128 * h:128 * h + 128], T.BO[:, ::16], True, True, ["FX", "BO"], ["B2"])
        for p in range(16):
            mm(T.B2[:, 16:32], qwin("QB", p), T.FX[:, p::16], p == 0, p == 15, ["QB", "FX"], ["B2"])
        mm(T.B3[:, 256:512], T.BO[:], T.FX[:], True, False, ["BO", "FX"], ["B3"])
        mm(T.B3[:, 256:512], T.ID2[:], T.NH[:], False, True, ["ID2", "NH"], ["B3"])
        mm(T.B7[:, 0:256], T.BOH[:], T.FH[:], True, False, ["BOH", "FH"], ["B7"])
        mm(T.B7[:, 0:256], T.ID128[:], T.NH[:], False, False, ["ID128", "NH"], ["B7"])
        ts(T.LF[:], T.B4[:, 0:16], 2048.0, OP.add, ["B4"], ["LF"])
        tt(T.SUB[:], T.LM[:, 0:W].indirect(T.LF[:, 0:16]), TM[:], OP.subtract, ["LM", "LF", M], ["SUB"])
        act(T.ABS[:], T.SUB[:], ["SUB"], ["ABS"], func=AF.Abs)
        tt(T.FC[:], T.LX[:, 0:W].indirect(T.LF[:, 0:16]), T.FB[:], OP.mult, ["LX", "LF", "FB"], ["FC"])
        act(T.SQ[:], T.B3[:, 256:512], ["B3", "SQB"], ["SQ"], func=AF.Square, bias=T.SQB[:])
        for h in range(2):
            s = slice(128 * h, 128 * h + 128)
            o = T.B4[:, 32 + 8 * h:40 + 8 * h]
            mm(o, T.FB[:, s], T.THB[:, ::16], True, False, ["FB", "THB"], ["B4"])
            mm(o, T.NH[:, s], T.BN8[:, ::16], False, False, ["NH", "BN8"], ["B4"])
            mm(o, T.ABS[:, s], T.BO[:, ::16], False, True, ["ABS", "BO"], ["B4"])
        for h in range(2):
            mm(T.B4[:, 16 + 8 * h:24 + 8 * h], T.FC[:, 128 * h:128 * h + 128], T.BO[:, ::16], True, True, ["FC", "BO"], ["B4"])
        cp(T.XTS[:], T.B2[:, 0:16], ["B2"], ["XTS"])
        cp(T.XL[:], T.B2[:, 16:32], ["B2"], ["XL"])
        for c in range(16):
            ts(T.OHX[:, 64 * c:64 * c + 64], T.IO64[:], T.XTS[:, c:c + 1], OP.is_equal, ["IO64", "XTS"], [("OHX", c // 4)])
        for p in range(16):
            mm(T.B2[:, 32:48], qwin("QB", p), T.FC[:, p::16], p == 0, p == 15, ["QB", "FC"], ["B2"])
        cp(T.CTS[:], T.B4[:, 16:32], ["B4"], ["CTS"])
        ts(T.NTS[:], T.B4[:, 32:48], 2047.5, OP.is_ge, ["B4"], ["NTS"])
        for c in range(16):
            s = slice(64 * c, 64 * c + 64)
            ts(T.OHC[:, s], T.IO64[:], T.CTS[:, c:c + 1], OP.is_equal, ["IO64", "CTS", "NTS"], [("OHC", c // 2)],
               T.NTS[:, c:c + 1], OP.mult)
            if c % 2 == 1:
                for d in (c - 1, c):
                    s = slice(64 * d, 64 * d + 64)
                    rd = [("OHX", d // 4), ("OHC", d // 2)]
                    mm(T.B5[0:64, 0:64], T.OHX[:, s], T.OHC[:, s], d == 0, False, rd, ["B5"])
                    mm(T.B5[0:64, 0:64], T.OHC[:, s], T.OHX[:, s], False, d == 15, rd, ["B5"])
        mm(T.B3[:, 0:256], T.THB[:], T.FB[:], True, False, ["THB", "FB"], ["B3"])
        mm(T.B3[:, 0:256], T.IDN128[:], T.NH[:], False, False, ["IDN128", "NH"], ["B3"])
        mm(T.B3[:, 0:256], T.BO[:], T.ABS[:], False, True, ["BO", "ABS"], ["B3"])
        ts(T.XL[:], T.XL[:], 3, OP.bitwise_and, ["XL"], ["XL"])
        ts(T.MK[:], T.SQ[:], 4.0, OP.is_le, ["SQ"], ["MK"])
        ts(T.XLF[:], T.XL[:], 64.0, OP.mult, ["XL"], ["XLF"])
        tt(T.CLF[:], T.XLF[:], T.B2[:, 32:48], OP.add, ["XLF", "B2"], ["CLF"])
        cp(T.CL[:], T.CLF[:], ["CLF"], ["CL"])
        ts(T.TB[0:64, :], T.B5[0:64, 0:64], 1.0, OP.min, ["B5"], ["TB"])
        for r in range(4):
            mm(T.B5[:, 256 + 64 * r:320 + 64 * r], T.RX[0:64, 128 * r:128 * r + 128], T.TB[0:64, :], True, True, ["RX", "TB"], ["B5"])
        act(T.TW[:], T.B5[:, 256:512], ["B5"], ["TW"])
        ts(T.HN[:], T.B3[:, 0:256], 2047.5, OP.is_ge, ["B3"], ["HN"])
        mm(T.B6[:, 0:256], T.ID[:], TX[:], True, False, ["ID", X], ["B6"])
        mm(T.B6[:, 0:256], T.IDN[:], T.FX[:], False, False, ["IDN", "FX"], ["B6"])
        mm(T.B6[:, 0:256], T.ID[:], T.FC[:], False, False, ["ID", "FC"], ["B6"])
        mm(T.B6[:, 0:256], T.ID64[:], T.HN[:], False, False, ["ID64", "HN"], ["B6"])
        mm(T.B7[:, 0:256], T.ID8192[:], T.HN[:], False, False, ["ID8192", "HN"], ["B7"])
        tt(T.GT[:], T.TW[:].indirect(T.CL[:, 0:16]), T.MK[:], OP.mult, ["TW", "CL", "MK"], ["GT"])
        mm(T.B6[:, 0:256], T.BO64[:], T.GT[:], False, True, ["BO64", "GT"], ["B6"])
        mm(T.B7[:, 0:256], T.BO8192[:], T.GT[:], False, True, ["BO8192", "GT"], ["B7"])
        tt(T[xn][:], T.XA[:], T.B6[:, 0:256], OP.min, ["XA", "B6"], [xn])
        dst = T.cores[(rank + (3 if t < 2 else 2)) % n_ranks]
        rid, pid, _eng = topo.addr(dst)
        mask = topo.mask(core, dst)
        ne = len(topo.engines(core, dst))

        def send(out, src, sem):
            before("g", [src], [])
            g.remote_dma(T[out][:], T[src][:], T.sem[sem], T.sem.ls, pid, rid, mask)
            lastw[out] = (sem, ne, {}, "remote")
        send("X%d" % (t + 1), xn, "ax%d" % (t + 1))
        ts(T.DK[:], T.B7[:, 0:256], 6144.0, OP.min, ["B7"], ["DK"])
        for p in range(16):
            mm(T.B4[:, 48:64], qwin("Q16", p), T.DK[:, p::16], p == 0, p == 15, ["Q16", "DK"], ["B4"])
        ts(T.MGR[:], T.B7[:, 0:256], 4000.0, OP.is_lt, ["B7"], ["MGR"])
        ts(T.DMI[:], T.SUB[:], 0.5, OP.mult, ["SUB"], ["DMI"], -0.25, OP.add)
        tt(T.DT[:], T.MGR[:], T.DMI[:], OP.mult, ["MGR", "DMI"], ["DT"])
        mm(T.B0[:, 0:256], T.ID[:], TM[:], True, False, ["ID", M], ["B0"])
        mm(T.B0[:, 0:256], T.ID[:], T.DT[:], False, True, ["ID", "DT"], ["B0"])
        act(T[mn][:], T.B0[:, 0:256], ["B0"], [mn])
        send("M%d" % (t + 1), mn, "am%d" % (t + 1))
        for p in range(16):
            mm(T.B5[:, 0:16], qwin("Q16", p), T.DK[:, p::16], p == 0, False, ["Q16", "DK"], ["B5"])
        cp(T.KLS[:], T.B4[:, 48:64], ["B4"], ["KLS"])
        for c in range(16):
            ts(T.EQ[:, c, 0:256 - 16 * c], T.DK[:, 16 * c:256], T.KLS[:, c:c + 1], OP.is_equal, ["DK", "KLS"], ["EQ"])
        tt(T.EQ[:, :, 0:16], T.EQ[:, :, 0:16], T.TRI[:], OP.mult, ["EQ", "TRI"], ["EQ"])
        for c in range(16):
            mm(T.B2[:, 16 * c:256], T.BO[:], T.EQ[:, c, 0:256 - 16 * c], c == 0, c == 15, ["BO", "EQ"], ["B2"])
        ts(T.LS[:], T.B2[:, 0:256], 0.5, OP.is_ge, ["B2"], ["LS"])
        for p in range(16):
            mm(T.B5[:, 0:16], qwin("Q512", p), T.LS[:, p::16], False, p == 15, ["Q512", "LS"], ["B5"])
        tt(T.OFF[:], T.B5[:, 0:16], T.IDX2[:], OP.min, ["B5", "IDX2"], ["OFF"])
        ts(T.OFU[:], T.OFF[:], 2048.0, OP.add, ["OFF"], ["OFU"])
        cp(T.LX[:].indirect(T.OFU[:, 0:16]), T[xn][:], ["OFU", xn, "LX"], ["LX"])

        def scatter_meanings(mn=mn):
            cp(T.LM[:].indirect(T.OFU[:, 0:16]), T[mn][:], ["OFU", mn, "LM"], ["LM"])
        deferred = [scatter_meanings]

    dma("s", T.yl[:], T.LX[:, 0:W], ["LX"], ["yl"])
    for f in deferred:
        f()
    act(T.CB[:, 0:1792], T.LM[:, 2304:4096], ["LM"], [("CB", 0), ("CB", 1)], accum_out=T.SUM[:, 1:2])
    lastw["SUM1"] = lastw[("CB", 0)]
    do("v", ["LM"], ["SUM0"], "reduce", out=T.SUM[:, 0:1], in_=T.LM[:, 0:2304], axis=AxisListType.X, op=OP.add)
    tt(T.YM[:], T.SUM[:, 0:1], T.SUM[:, 1:2], OP.add, ["SUM0", "SUM1"], ["YM"])
    dma("y", T.yx[:], T.X3[:], ["X3"], ["yx"])
    dma("y", T.yg[:], T.M3[:], ["M3"], ["yg"])
    dma("y", T.ym[:], T.YM[:], ["YM"], ["ym"])
    for sem in ("qv", "qs", "qt", "qg"):
        wait("g", (sem, count[sem], {}, ""))
    for tok in dmas:
        wait("g", tok)
    for s in range(1, 4):
        wait("g", ("ax%d" % s, ne, {}, ""))
        wait("g", ("am%d" % s, ne, {}, ""))
    g.wait_ge(T.sem.ls, 6 * ne)
